import numpy as np
import ml_dtypes


def mxq(x, axis, fmt="e4m3"):
    dtype, down = {"e4m3": (ml_dtypes.float8_e4m3fn, 7), "e5m2": (ml_dtypes.float8_e5m2, 14)}[fmt]
    v = np.moveaxis(np.asarray(x, np.float32).astype(ml_dtypes.bfloat16).astype(np.float64), axis, -1)
    blocks = v.reshape(v.shape[:-1] + (-1, 32))
    amax = np.abs(blocks).max(-1, keepdims=True)
    byte = np.maximum(np.where(amax > 0, np.frexp(amax)[1] - 1 + 127, 0) - down, 1)
    scale = np.exp2(byte - 127.0)
    codes = (blocks / scale).astype(np.float32).astype(dtype).astype(np.float64)
    return np.moveaxis((codes * scale).reshape(v.shape), -1, axis)


WIDE = False


def mx_kscale(k):
    if not WIDE:
        return np.ones(k)
    levels = np.array([10, -10, 5, -5, 0])
    if k % 512:
        return np.exp2(np.random.permutation(np.resize(levels, k // 32))).repeat(32)
    a = np.empty((k // 512, 16))
    for p in range(k // 512):
        a[p, :8] = np.random.permutation(np.resize(levels, 8))
        for g in range(8):
            far = levels[np.abs(levels - a[p, g]) >= 10]
            a[p, g + 8] = far[np.random.randint(len(far))]
    return np.exp2(a.ravel()).repeat(32)


def f64(x):
    return np.asarray(x).astype(np.float64)


def striped8(idx):
    return np.asarray(idx).reshape(8, -1, 16).transpose(0, 2, 1).reshape(128, -1).astype(np.uint16)


def unstriped8(offs):
    return offs.reshape(8, 16, -1).transpose(0, 2, 1).reshape(8, -1).astype(np.int64)


def pick8(x, idx, run):
    r = np.arange(len(x))
    return x[r[:, None], idx[r % (8 * run) // run]]


E2M1 = np.array([0.0, 0.5, 1.0, 1.5, 2.0, 3.0, 4.0, 6.0, -0.0, -0.5, -1.0, -1.5, -2.0, -3.0, -4.0, -6.0])


def pack_weight(w, fmt):
    k, n = w.shape
    w = f64(np.asarray(w, np.float32).astype(ml_dtypes.bfloat16)).reshape(k // 32, 32, n)
    amax = np.abs(w).max(1)
    if fmt == "e4m3":
        byte = np.frexp(amax)[1] - 1 + 127 - 7
    else:
        mant, ex = np.frexp(amax / 6.0)
        byte = np.where(mant > 0.5, ex, ex - 1) + 127
    byte = np.clip(np.where(amax > 0, byte, 1), 1, 254)
    scaled = (w * np.exp2(127.0 - byte)[:, None, :]).reshape(k, n).astype(np.float32)
    by_word = np.ascontiguousarray(scaled.reshape(k // 512, 128, 4, n).transpose(0, 1, 3, 2))
    if fmt == "e4m3":
        words = by_word.astype(ml_dtypes.float8_e4m3fn).view(np.uint8)
    else:
        c = by_word.astype(ml_dtypes.float4_e2m1fn).view(np.uint8) & 0xF
        words = (c[..., 0::2] | (c[..., 1::2] << 4)).reshape(k // 512, 128, 2 * n)
    return np.ascontiguousarray(words), np.ascontiguousarray(byte.astype(np.uint8).reshape(k // 512, 16, n))


def unpack_weight(words, scales, fmt):
    g, _, n = scales.shape
    words = np.ascontiguousarray(words).reshape(g, 128, n, -1)
    if fmt == "e4m3":
        vals = words.view(ml_dtypes.float8_e4m3fn).astype(np.float64)
    else:
        nib = np.empty((g, 128, n, 4), np.uint8)
        nib[..., 0::2] = words & 0xF
        nib[..., 1::2] = words >> 4
        vals = E2M1[nib]
    vals = vals * np.repeat(np.exp2(scales.astype(np.float64) - 127.0), 8, axis=1)[..., None]
    return vals.transpose(0, 1, 3, 2).reshape(g * 512, n)


D, T, I, Q = 512, 1024, 512, 128


def setup_inputs():
    n = np.random.standard_normal
    idx = np.stack([np.random.permutation(T)[:I] for _ in range(8)])
    idx2 = np.stack([np.random.permutation(T)[:I] for _ in range(8)])
    idx3 = np.stack([np.random.permutation(T)[:I] for _ in range(8)])
    idx4 = np.stack([np.random.permutation(T)[:I] for _ in range(8)])
    fd = mx_kscale(D)
    keysp = pack_weight(n((D, T)) / fd[:, None], "e4m3")
    tagsp = pack_weight(n((D, T)) / fd[:, None], "e2m1")
    return {
        "query": (n((D, Q)) * 0.75 / np.sqrt(D) * fd[:, None]).astype(np.float32),
        "query2": (n((D, Q)) * 0.75 / np.sqrt(D) * fd[:, None]).astype(np.float32),
        "keys_words": keysp[0],
        "keys_scales": keysp[1],
        "tags_words": tagsp[0],
        "tags_scales": tagsp[1],
        "offs": striped8(idx),
        "offs2": striped8(idx2),
        "offs3": striped8(idx3),
        "offs4": striped8(idx4),
    }


def reference(query, query2, keys_words, keys_scales, tags_words, tags_scales, offs, offs2, offs3, offs4):
    idx = unstriped8(offs)
    idx2 = unstriped8(offs2)
    idx3 = unstriped8(offs3)
    idx4 = unstriped8(offs4)
    keysu = unpack_weight(keys_words, keys_scales, "e4m3")
    tagsu = unpack_weight(tags_words, tags_scales, "e2m1")
    queryq = mxq(f64(query), 0, "e4m3")
    query2q = mxq(f64(query2), 0, "e4m3")
    a = queryq.T @ keysu + query2q.T @ tagsu
    ta = np.max(a, axis=1, keepdims=True)
    e1 = np.exp(pick8(a, idx, 16) - ta)
    f1 = np.zeros((Q, T))
    f1[np.arange(Q)[:, None], idx2[np.arange(Q) % 128 // 16]] = e1
    f2 = np.zeros((Q, T))
    f2[np.arange(Q)[:, None], idx3[np.arange(Q) % 128 // 16]] = e1
    r = f1 - f2
    cc = a + r * 4.0
    y = pick8(cc, idx4, 16)
    return y

@@ -1,0 +1,130 @@
+from contextlib import ExitStack
+
+import concourse.mybir as mybir
+from concourse.masks import make_identity
+
+F32 = mybir.dt.float32
+BF16 = mybir.dt.bfloat16
+I32 = mybir.dt.int32
+U32 = mybir.dt.uint32
+U16 = mybir.dt.uint16
+U8 = mybir.dt.uint8
+FP8X4 = mybir.dt.float8_e4m3fn_x4
+FP4X4 = mybir.dt.float4_e2m1fn_x4
+ALU = mybir.AluOpType
+ACT = mybir.ActivationFunctionType
+
+P = 128
+D, T, I, Q = 512, 1024, 512, 128
+CH = 256
+NCH = T // CH
+FLOPS = 2 * 2 * D * Q * T
+
+
+def tile_attend_giveandtake_parts_kernel(tc, query, query2, keys_words, keys_scales, tags_words, tags_scales,
+                                          offs, offs2, offs3, offs4, out):
+    nc = tc.nc
+    with ExitStack() as ctx:
+        held = ctx.enter_context(tc.tile_pool(name="held", bufs=1))
+        psum = ctx.enter_context(tc.psum_pool(name="psum", bufs=1))
+        lists = [held.tile([P, I // 16], U16, name="list%d" % k) for k in range(4)]
+
+        planes = [held.tile([P, T], U8, name="plane%d" % k, align_bytes=64) for k in range(2)]
+        for k in (1, 0):
+            nc.vector.memset(planes[k][:].bitcast(I32), 0)
+        f1 = [held.tile([P, T], F32, name="f1_%d" % h) for h in range(2)]
+        for h in range(2):
+            nc.vector.memset(f1[h][:], 0.0)
+
+        raw = [held.tile([P, 4, Q], F32, name="raw%d" % k) for k in range(2)]
+        tags = held.tile([P, 2 * T], U8, name="tags", align_bytes=64)
+        keys = [held.tile([P, T // 2], I32, name="keys%d" % h, align_bytes=64) for h in range(2)]
+        kw = keys_words[0].rearrange("p n t -> p (n t)")
+
+        def load_scale_rows(queue, plane, first, src, r):
+            queue.dma_start(out=plane[:].bitcast(I32)[first + r:P:32, :], in_=src[0].bitcast(I32)[r:16:4, :])
+
+        def load_keys(queue, h):
+            queue.dma_start(out=keys[h][:], in_=kw[:, 2 * T * h:2 * T * (h + 1)].bitcast(I32))
+
+        queues = (nc.scalar, nc.sync)
+        nc.sync.dma_start(out=raw[1][:], in_=query2.rearrange("(p j) q -> p j q", j=4))
+        for r in range(4):
+            load_scale_rows(queues[r % 2], planes[1], 0, tags_scales, r)
+        nc.scalar.dma_start(out=raw[0][:], in_=query.rearrange("(p j) q -> p j q", j=4))
+        nc.sync.dma_start(out=tags[:].bitcast(I32), in_=tags_words[0].bitcast(I32))
+        load_keys(nc.scalar, 0)
+        load_keys(nc.sync, 1)
+        for r in range(4):
+            load_scale_rows(queues[r % 2], planes[0], 4, keys_scales, r)
+        for k, src in enumerate((offs, offs2, offs3, offs4)):
+            nc.sync.dma_start(lists[k][:], src)
+        ident = held.tile([P, P], F32, name="ident")
+        make_identity(nc, ident[:])
+
+        codes, scales = [], []
+        for k in range(2):
+            codes.append(held.tile([P, Q], U32, name="codes%d" % k, align_bytes=64))
+            scales.append(held.tile([P, Q], U8, name="scales%d" % k, align_bytes=64))
+        for k in (1, 0):
+            grouped = held.tile([P, Q, 4], BF16, name="grouped%d" % k, tag="shared%d" % k, align_bytes=64)
+            nc.vector.tensor_copy(out=grouped[:], in_=raw[k][:].rearrange("p j q -> p q j"))
+            nc.vector.quantize_mx(out=codes[k][:].bitcast(FP8X4), scales=scales[k][:],
+                                  in_=grouped[:].rearrange("p q j -> p (q j)"))
+
+        f2 = held.tile([P, T], F32, name="f2", tag="shared0", align_bytes=64)
+        nc.gpsimd.memset(f2[:], 0.0)
+        banks = [psum.tile([P, CH], F32, name="bank%d" % c) for c in range(NCH)]
+        for c in range(NCH):
+            nc.tensor.matmul_mx(out=banks[c][:], lhsT=codes[1][:].bitcast(FP8X4), lhsT_scale=scales[1][:],
+                                rhs=tags[:, 2 * CH * c:2 * CH * (c + 1)].bitcast(FP4X4),
+                                rhs_scale=planes[1][:, CH * c:CH * (c + 1)], start=True, stop=False)
+        a = held.tile([P, T], F32, name="a")
+        tops = held.tile([P, NCH], F32, name="tops")
+        for c in range(NCH):
+            kc = keys[c // 2][:, CH * (c % 2):CH * (c % 2 + 1)]
+            nc.tensor.matmul_mx(out=banks[c][:], lhsT=codes[0][:].bitcast(FP8X4), lhsT_scale=scales[0][:],
+                                rhs=kc.bitcast(FP8X4), rhs_scale=planes[0][4:P, CH * c:CH * (c + 1)],
+                                start=False, stop=True)
+            nc.vector.tensor_scalar(out=a[:, CH * c:CH * (c + 1)], in0=banks[c][:], scalar1=1.0, scalar2=None,
+                                    op0=ALU.mult, op1=ALU.max, accum_out=tops[:, c:c + 1])
+        neg_top = held.tile([P, 1], F32, name="neg_top")
+        nc.vector.tensor_reduce(out=neg_top[:], in_=tops[:], axis=mybir.AxisListType.X, op=ALU.max, negate=True)
+
+        H = I // 2
+        e1 = held.tile([P, I], F32, name="e1")
+        for h in range(2):
+            nc.scalar.activation(out=e1[:, H * h:H * (h + 1)], in_=a[:].indirect(lists[0][:, 16 * h:16 * (h + 1)]), func=ACT.Exp,
+                                 bias=neg_top[:])
+        quarter = held.tile([P, T], F32, name="quarter")
+        nc.vector.tensor_scalar(out=quarter[:], in0=a[:], scalar1=0.25, scalar2=None, op0=ALU.mult)
+        turned = [psum.tile([P, 4, P], F32, name="turned%d" % b) for b in range(2)]
+        for b in range(2):
+            for j in range(4):
+                col = 512 * b + P * j
+                nc.tensor.matmul(out=turned[b][:, j, :], lhsT=quarter[:, col:col + P], rhs=ident[:],
+                                 start=(j == 0), stop=False, is_transpose=True)
+        for h in range(2):
+            nc.vector.tensor_copy(out=f1[h][:].indirect(lists[1][:, 16 * h:16 * (h + 1)]), in_=e1[:, H * h:H * (h + 1)])
+        nc.vector.tensor_copy(out=f2[:].indirect(lists[2][:]), in_=e1[:])
+        for h in range(2):
+            for b in range(2):
+                for j in range(4):
+                    col = 512 * b + P * j
+                    nc.tensor.matmul(out=turned[b][:, j, :], lhsT=f1[h][:, col:col + P], rhs=ident[:],
+                                     start=False, stop=(h == 1 and j == 3), is_transpose=True)
+        cc = held.tile([P, T], F32, name="cc")
+        for b in range(2):
+            given_t = held.tile([P, 4, P], F32, name="given_t%d" % b)
+            nc.scalar.activation(out=given_t[:], in_=turned[b][:], func=ACT.Copy, scale=4.0)
+            given = psum.tile([P, 4 * P], F32, name="given%d" % b)
+            for j in range(4):
+                nc.tensor.transpose(given[:, P * j:P * (j + 1)], given_t[:, j, :], ident[:])
+            cols = slice(512 * b, 512 * (b + 1))
+            nc.vector.scalar_tensor_tensor(out=cc[:, cols], in0=f2[:, cols], scalar=-4.0, in1=given[:],
+                                           op0=ALU.mult, op1=ALU.add)
+        y = [held.tile([P, H], F32, name="y%d" % h) for h in range(2)]
+        nc.vector.tensor_copy(out=y[0][:], in_=cc[:].indirect(lists[3][:, 0:16]))
+        nc.scalar.activation(out=y[1][:], in_=cc[:].indirect(lists[3][:, 16:32]), func=ACT.Copy)
+        nc.sync.dma_start(out=out[:, 0:H], in_=y[0][:])
+        nc.scalar.dma_start(out=out[:, H:I], in_=y[1][:])

@@ -30,8 +30,8 @@ def tile_attend_giveandtake_parts_kernel(tc, query, query2, keys_words, keys_sca
         lists = [held.tile([P, I // 16], U16, name="list%d" % k) for k in range(4)]
 
         planes = [held.tile([P, T], U8, name="plane%d" % k, align_bytes=64) for k in range(2)]
-        for k in (1, 0):
-            nc.vector.memset(planes[k][:].bitcast(I32), 0)
+        nc.gpsimd.memset(planes[1][:].bitcast(I32), 0)
+        nc.vector.memset(planes[0][:].bitcast(I32), 0)
         f1 = [held.tile([P, T], F32, name="f1_%d" % h) for h in range(2)]
         for h in range(2):
             nc.vector.memset(f1[h][:], 0.0)
@@ -44,19 +44,15 @@ def tile_attend_giveandtake_parts_kernel(tc, query, query2, keys_words, keys_sca
         def load_scale_rows(queue, plane, first, src, r):
             queue.dma_start(out=plane[:].bitcast(I32)[first + r:P:32, :], in_=src[0].bitcast(I32)[r:16:4, :])
 
-        def load_keys(queue, h):
-            queue.dma_start(out=keys[h][:], in_=kw[:, 2 * T * h:2 * T * (h + 1)].bitcast(I32))
-
-        queues = (nc.scalar, nc.sync)
         nc.sync.dma_start(out=raw[1][:], in_=query2.rearrange("(p j) q -> p j q", j=4))
-        for r in range(4):
-            load_scale_rows(queues[r % 2], planes[1], 0, tags_scales, r)
-        nc.scalar.dma_start(out=raw[0][:], in_=query.rearrange("(p j) q -> p j q", j=4))
+        for r, queue in enumerate((nc.scalar, nc.sync, nc.scalar, nc.sync)):
+            load_scale_rows(queue, planes[1], 0, tags_scales, r)
         nc.sync.dma_start(out=tags[:].bitcast(I32), in_=tags_words[0].bitcast(I32))
-        load_keys(nc.scalar, 0)
-        load_keys(nc.sync, 1)
+        nc.sync.dma_start(out=raw[0][:], in_=query.rearrange("(p j) q -> p j q", j=4))
+        nc.sync.dma_start(out=keys[0][:], in_=kw[:, 0:2 * T].bitcast(I32))
         for r in range(4):
-            load_scale_rows(queues[r % 2], planes[0], 4, keys_scales, r)
+            load_scale_rows(nc.sync, planes[0], 4, keys_scales, r)
+        nc.sync.dma_start(out=keys[1][:], in_=kw[:, 2 * T:4 * T].bitcast(I32))
         for k, src in enumerate((offs, offs2, offs3, offs4)):
             nc.sync.dma_start(lists[k][:], src)
         ident = held.tile([P, P], F32, name="ident")
@@ -68,7 +64,10 @@ def tile_attend_giveandtake_parts_kernel(tc, query, query2, keys_words, keys_sca
             scales.append(held.tile([P, Q], U8, name="scales%d" % k, align_bytes=64))
         for k in (1, 0):
             grouped = held.tile([P, Q, 4], BF16, name="grouped%d" % k, tag="shared%d" % k, align_bytes=64)
-            nc.vector.tensor_copy(out=grouped[:], in_=raw[k][:].rearrange("p j q -> p q j"))
+            dst = grouped[:].rearrange("p (c i) j -> p c j i", i=4)
+            src = raw[k][:].rearrange("p j (c i) -> p c j i", i=4)
+            nc.vector.tensor_copy(out=dst[:, 0:16], in_=src[:, 0:16])
+            nc.scalar.activation(out=dst[:, 16:32], in_=src[:, 16:32], func=ACT.Copy)
             nc.vector.quantize_mx(out=codes[k][:].bitcast(FP8X4), scales=scales[k][:],
                                   in_=grouped[:].rearrange("p q j -> p (q j)"))
 

from contextlib import ExitStack

import concourse.mybir as mybir
from concourse.masks import make_identity

F32 = mybir.dt.float32
BF16 = mybir.dt.bfloat16
I32 = mybir.dt.int32
U32 = mybir.dt.uint32
U16 = mybir.dt.uint16
U8 = mybir.dt.uint8
FP8X4 = mybir.dt.float8_e4m3fn_x4
FP4X4 = mybir.dt.float4_e2m1fn_x4
ALU = mybir.AluOpType
ACT = mybir.ActivationFunctionType

P = 128
D, T, I, Q = 512, 1024, 512, 128
CH = 256
NCH = T // CH
FLOPS = 2 * 2 * D * Q * T


def tile_attend_giveandtake_parts_kernel(tc, query, query2, keys_words, keys_scales, tags_words, tags_scales,
                                          offs, offs2, offs3, offs4, out):
    nc = tc.nc
    with ExitStack() as ctx:
        held = ctx.enter_context(tc.tile_pool(name="held", bufs=1))
        psum = ctx.enter_context(tc.psum_pool(name="psum", bufs=1))
        lists = [held.tile([P, I // 16], U16, name="list%d" % k) for k in range(4)]

        planes = [held.tile([P, T], U8, name="plane%d" % k, align_bytes=64) for k in range(2)]
        nc.gpsimd.memset(planes[1][:].bitcast(I32), 0)
        nc.vector.memset(planes[0][:].bitcast(I32), 0)
        f1 = [held.tile([P, T], F32, name="f1_%d" % h) for h in range(2)]
        for h in range(2):
            nc.vector.memset(f1[h][:], 0.0)

        raw = [held.tile([P, 4, Q], F32, name="raw%d" % k) for k in range(2)]
        tags = held.tile([P, 2 * T], U8, name="tags", align_bytes=64)
        keys = [held.tile([P, T // 2], I32, name="keys%d" % h, align_bytes=64) for h in range(2)]
        kw = keys_words[0].rearrange("p n t -> p (n t)")

        def load_scale_rows(queue, plane, first, src, r):
            queue.dma_start(out=plane[:].bitcast(I32)[first + r:P:32, :], in_=src[0].bitcast(I32)[r:16:4, :])

        nc.sync.dma_start(out=raw[1][:], in_=query2.rearrange("(p j) q -> p j q", j=4))
        for r, queue in enumerate((nc.scalar, nc.sync, nc.scalar, nc.sync)):
            load_scale_rows(queue, planes[1], 0, tags_scales, r)
        nc.sync.dma_start(out=tags[:].bitcast(I32), in_=tags_words[0].bitcast(I32))
        nc.sync.dma_start(out=raw[0][:], in_=query.rearrange("(p j) q -> p j q", j=4))
        nc.sync.dma_start(out=keys[0][:], in_=kw[:, 0:2 * T].bitcast(I32))
        for r in range(4):
            load_scale_rows(nc.sync, planes[0], 4, keys_scales, r)
        nc.sync.dma_start(out=keys[1][:], in_=kw[:, 2 * T:4 * T].bitcast(I32))
        for k, src in enumerate((offs, offs2, offs3, offs4)):
            nc.sync.dma_start(lists[k][:], src)
        ident = held.tile([P, P], F32, name="ident")
        make_identity(nc, ident[:])

        codes, scales = [], []
        for k in range(2):
            codes.append(held.tile([P, Q], U32, name="codes%d" % k, align_bytes=64))
            scales.append(held.tile([P, Q], U8, name="scales%d" % k, align_bytes=64))
        for k in (1, 0):
            grouped = held.tile([P, Q, 4], BF16, name="grouped%d" % k, tag="shared%d" % k, align_bytes=64)
            dst = grouped[:].rearrange("p (c i) j -> p c j i", i=4)
            src = raw[k][:].rearrange("p j (c i) -> p c j i", i=4)
            nc.vector.tensor_copy(out=dst[:, 0:16], in_=src[:, 0:16])
            nc.scalar.activation(out=dst[:, 16:32], in_=src[:, 16:32], func=ACT.Copy)
            nc.vector.quantize_mx(out=codes[k][:].bitcast(FP8X4), scales=scales[k][:],
                                  in_=grouped[:].rearrange("p q j -> p (q j)"))

        f2 = held.tile([P, T], F32, name="f2", tag="shared0", align_bytes=64)
        nc.gpsimd.memset(f2[:], 0.0)
        banks = [psum.tile([P, CH], F32, name="bank%d" % c) for c in range(NCH)]
        for c in range(NCH):
            nc.tensor.matmul_mx(out=banks[c][:], lhsT=codes[1][:].bitcast(FP8X4), lhsT_scale=scales[1][:],
                                rhs=tags[:, 2 * CH * c:2 * CH * (c + 1)].bitcast(FP4X4),
                                rhs_scale=planes[1][:, CH * c:CH * (c + 1)], start=True, stop=False)
        a = held.tile([P, T], F32, name="a")
        tops = held.tile([P, NCH], F32, name="tops")
        for c in range(NCH):
            kc = keys[c // 2][:, CH * (c % 2):CH * (c % 2 + 1)]
            nc.tensor.matmul_mx(out=banks[c][:], lhsT=codes[0][:].bitcast(FP8X4), lhsT_scale=scales[0][:],
                                rhs=kc.bitcast(FP8X4), rhs_scale=planes[0][4:P, CH * c:CH * (c + 1)],
                                start=False, stop=True)
            nc.vector.tensor_scalar(out=a[:, CH * c:CH * (c + 1)], in0=banks[c][:], scalar1=1.0, scalar2=None,
                                    op0=ALU.mult, op1=ALU.max, accum_out=tops[:, c:c + 1])
        neg_top = held.tile([P, 1], F32, name="neg_top")
        nc.vector.tensor_reduce(out=neg_top[:], in_=tops[:], axis=mybir.AxisListType.X, op=ALU.max, negate=True)

        H = I // 2
        e1 = held.tile([P, I], F32, name="e1")
        for h in range(2):
            nc.scalar.activation(out=e1[:, H * h:H * (h + 1)], in_=a[:].indirect(lists[0][:, 16 * h:16 * (h + 1)]), func=ACT.Exp,
                                 bias=neg_top[:])
        quarter = held.tile([P, T], F32, name="quarter")
        nc.vector.tensor_scalar(out=quarter[:], in0=a[:], scalar1=0.25, scalar2=None, op0=ALU.mult)
        turned = [psum.tile([P, 4, P], F32, name="turned%d" % b) for b in range(2)]
        for b in range(2):
            for j in range(4):
                col = 512 * b + P * j
                nc.tensor.matmul(out=turned[b][:, j, :], lhsT=quarter[:, col:col + P], rhs=ident[:],
                                 start=(j == 0), stop=False, is_transpose=True)
        for h in range(2):
            nc.vector.tensor_copy(out=f1[h][:].indirect(lists[1][:, 16 * h:16 * (h + 1)]), in_=e1[:, H * h:H * (h + 1)])
        nc.vector.tensor_copy(out=f2[:].indirect(lists[2][:]), in_=e1[:])
        for h in range(2):
            for b in range(2):
                for j in range(4):
                    col = 512 * b + P * j
                    nc.tensor.matmul(out=turned[b][:, j, :], lhsT=f1[h][:, col:col + P], rhs=ident[:],
                                     start=False, stop=(h == 1 and j == 3), is_transpose=True)
        cc = held.tile([P, T], F32, name="cc")
        for b in range(2):
            given_t = held.tile([P, 4, P], F32, name="given_t%d" % b)
            nc.scalar.activation(out=given_t[:], in_=turned[b][:], func=ACT.Copy, scale=4.0)
            given = psum.tile([P, 4 * P], F32, name="given%d" % b)
            for j in range(4):
                nc.tensor.transpose(given[:, P * j:P * (j + 1)], given_t[:, j, :], ident[:])
            cols = slice(512 * b, 512 * (b + 1))
            nc.vector.scalar_tensor_tensor(out=cc[:, cols], in0=f2[:, cols], scalar=-4.0, in1=given[:],
                                           op0=ALU.mult, op1=ALU.add)
        y = [held.tile([P, H], F32, name="y%d" % h) for h in range(2)]
        nc.vector.tensor_copy(out=y[0][:], in_=cc[:].indirect(lists[3][:, 0:16]))
        nc.scalar.activation(out=y[1][:], in_=cc[:].indirect(lists[3][:, 16:32]), func=ACT.Copy)
        nc.sync.dma_start(out=out[:, 0:H], in_=y[0][:])
        nc.scalar.dma_start(out=out[:, H:I], in_=y[1][:])
